import numpy as np
import ml_dtypes


def mxq(x, axis, fmt="e4m3"):
    dtype, down = {"e4m3": (ml_dtypes.float8_e4m3fn, 7), "e5m2": (ml_dtypes.float8_e5m2, 14)}[fmt]
    v = np.moveaxis(np.asarray(x, np.float32).astype(ml_dtypes.bfloat16).astype(np.float64), axis, -1)
    blocks = v.reshape(v.shape[:-1] + (-1, 32))
    amax = np.abs(blocks).max(-1, keepdims=True)
    byte = np.maximum(np.where(amax > 0, np.frexp(amax)[1] - 1 + 127, 0) - down, 1)
    scale = np.exp2(byte - 127.0)
    codes = (blocks / scale).astype(np.float32).astype(dtype).astype(np.float64)
    return np.moveaxis((codes * scale).reshape(v.shape), -1, axis)


WIDE = False


def mx_kscale(k):
    if not WIDE:
        return np.ones(k)
    levels = np.array([30, -30])
    if k % 512:
        return np.exp2(np.random.permutation(np.resize(levels, k // 32))).repeat(32)
    a = np.empty((k // 512, 16))
    for p in range(k // 512):
        a[p, :8] = np.random.permutation(np.resize(levels, 8))
        for g in range(8):
            far = levels[np.abs(levels - a[p, g]) >= 10]
            a[p, g + 8] = far[np.random.randint(len(far))]
    return np.exp2(a.ravel()).repeat(32)


def f64(x):
    return np.asarray(x).astype(np.float64)


def striped(idx):
    return np.tile(idx.reshape(-1, 16).T, (8, 1)).astype(np.uint16)


def unstriped(offs):
    return offs[:16].T.reshape(-1).astype(np.int64)


K, T, E, C, N = 256, 1024, 4, 512, 1536


def by_expert(wq, xq):
    return np.concatenate([wq[e].T @ xq[:, e * C:(e + 1) * C] for e in range(E)], axis=1)


def setup_inputs():
    n = np.random.standard_normal
    s = mx_kscale(N)[:, None]
    first = np.random.permutation(np.repeat(np.arange(E), T // E))
    second = (first + 1 + np.random.permutation(np.repeat(np.arange(E - 1), -(-T // (E - 1)))[:T])) % E
    while np.bincount(second, minlength=E).max() != T // E:
        load = np.bincount(second, minlength=E); hi, lo = int(load.argmax()), int(load.argmin())
        t = np.flatnonzero((second == hi) & (first != lo))[0]; second[t] = lo
    slot_token = np.empty(E * C, np.int64); pos = np.empty((2, T), np.int64); fill = np.zeros(E, np.int64)
    place = np.stack([np.random.permutation(C) for _ in range(E)])
    for r, deal in enumerate((first, second)):
        for t in np.random.permutation(T):
            e = deal[t]; j = e * C + place[e, fill[e]]; fill[e] += 1; slot_token[j] = t; pos[r, t] = j
    g = np.random.uniform(0.2, 0.8, T)
    w_slot = np.empty(E * C); w_slot[pos[0]] = g; w_slot[pos[1]] = 1.0 - g
    return {
        "dyT": (n((N, T)) * s).astype(np.float32),
        "w": (n((E + 1, N, K)) / np.sqrt(N) / s[None]).astype(np.float32),
        "gate": np.tile(w_slot, (N, 1)).astype(np.float32),
        "offs": striped(slot_token),
        "pos1": striped(pos[0]),
        "pos2": striped(pos[1]),
    }


def reference(dyT, w, gate, offs, pos1, pos2):
    idx = unstriped(offs)
    gq = mxq(f64(gate) * f64(dyT)[:, idx], 0, "e5m2")
    wq = mxq(f64(w), 1, "e4m3")
    ds = wq[E].T @ mxq(f64(dyT), 0, "e5m2")
    dx = by_expert(wq, gq)
    return ds + dx[:, unstriped(pos1)] + dx[:, unstriped(pos2)]

@@ -1,0 +1,224 @@
+from contextlib import ExitStack
+
+import concourse.mybir as mybir
+
+K, T, E, C, N = 256, 1024, 4, 512, 1536
+SLOTS = E * C
+FLOPS = 2 * N * K * (SLOTS + T)
+BYTES = 4 * (N * T + (E + 1) * N * K + SLOTS + K * T) + 2 * 128 * (SLOTS + 2 * T) // 16
+
+F32 = mybir.dt.float32
+BF16 = mybir.dt.bfloat16
+U32 = mybir.dt.uint32
+U16 = mybir.dt.uint16
+U8 = mybir.dt.uint8
+E4M3 = mybir.dt.float8_e4m3fn_x4
+E5M2 = mybir.dt.float8_e5m2_x4
+MULT = mybir.AluOpType.mult
+ADD = mybir.AluOpType.add
+
+P = 128
+PACK = 4
+PASS_ROWS = P * PACK
+PASSES = N // PASS_ROWS
+K_TILES = K // P
+HALF = 512
+STRIPE = 16
+RUN = 4
+
+
+def tile_moe_bds_lin_none_kernel(tc, dyT, w, gate, offs, pos1, pos2, out):
+    nc = tc.nc
+    with ExitStack() as ctx:
+        lists = ctx.enter_context(tc.tile_pool(name="lists", bufs=1))
+        keep = ctx.enter_context(tc.tile_pool(name="keep", bufs=1))
+        ring = ctx.enter_context(tc.tile_pool(name="ring", bufs=1))
+        psum = ctx.enter_context(tc.psum_pool(name="psum", bufs=1))
+
+        offs_t = lists.tile([P, SLOTS // STRIPE], U16, name="offs_t")
+        pos1_t = lists.tile([P, T // STRIPE], U16, name="pos1_t")
+        pos2_t = lists.tile([P, T // STRIPE], U16, name="pos2_t")
+        dx = [keep.tile([P, SLOTS], F32, name="dx%d" % kt) for kt in range(K_TILES)]
+
+        planes, gates, w_raw, w_bf, w_mx = {}, {}, {}, {}, {}
+        g_raw, g_bf, g_mx, banks = {}, {}, {}, {}
+        s_raw, s_bf, s_mx, ds_banks = {}, {}, {}, {}
+
+        def pass_rows(mat, c):
+            return mat[c * PASS_ROWS : (c + 1) * PASS_ROWS, :].rearrange("(p j) x -> p j x", j=PACK)
+
+        def load_plane(c, j):
+            planes[c, j] = ring.tile([P, T], F32, name="plane", bufs=8)
+            nc.sync.dma_start(planes[c, j][:], pass_rows(dyT, c)[:, j, :])
+
+        def load_gate(e):
+            gates[e] = keep.tile([P, C], F32, name="gate%d" % e)
+            nc.sync.dma_start(gates[e][:], gate[0:P, e * C : (e + 1) * C])
+
+        def load_w(c, e):
+            w_raw[c, e] = ring.tile([P, PACK, K], F32, name="w_raw", bufs=5)
+            nc.sync.dma_start(w_raw[c, e][:], pass_rows(w[e], c))
+
+        def load_shared(c, h):
+            s_raw[c, h] = ring.tile([P, PACK, HALF], F32, name="s_raw", bufs=2)
+            nc.sync.dma_start(s_raw[c, h][:], pass_rows(dyT, c)[:, :, h * HALF : (h + 1) * HALF])
+
+        def interleave(dst, src):
+            nc.scalar.copy(
+                dst[:].rearrange("p (c i) j -> p c j i", i=RUN),
+                src[:].rearrange("p j (c i) -> p c j i", i=RUN),
+            )
+
+        def quantize(codes, scales, src, fmt):
+            nc.vector.quantize_mx(out=codes.bitcast(fmt), scales=scales, in_=src[:].rearrange("p x j -> p (x j)"))
+
+        def mx_tiles(width, name, bufs):
+            codes = ring.tile([P, width], U32, name=name + "_codes", bufs=bufs, align_bytes=64)
+            scales = ring.tile([P, width], U8, name=name + "_scales", bufs=bufs, align_bytes=64)
+            return codes, scales
+
+        def round_w(c, e):
+            tag, bufs = ("ws_bf", PASSES) if e == E else ("w_bf", 3)
+            w_bf[c, e] = ring.tile([P, K, PACK], BF16, name=tag, bufs=bufs, align_bytes=64)
+            interleave(w_bf[c, e], w_raw[c, e])
+
+        def quantize_w(c, e):
+            w_mx[c, e] = mx_tiles(K, "ws", PASSES) if e == E else mx_tiles(K, "w", 3)
+            quantize(w_mx[c, e][0][:], w_mx[c, e][1][:], w_bf[c, e], E4M3)
+
+        def round_shared(c, h):
+            s_bf[c, h] = ring.tile([P, HALF, PACK], BF16, name="s_bf", bufs=4, align_bytes=64)
+            interleave(s_bf[c, h], s_raw[c, h])
+
+        def quantize_shared(c, h):
+            s_mx[c, h] = mx_tiles(HALF, "s", 2 * PASSES)
+            quantize(s_mx[c, h][0][:], s_mx[c, h][1][:], s_bf[c, h], E5M2)
+
+        def gather_g(c, e, lo, hi):
+            g_raw[c, e, lo] = ring.tile([P, PACK, hi - lo], F32, name="g_raw", bufs=3)
+            picks = offs_t[:, (e * C + lo) // STRIPE : (e * C + hi) // STRIPE]
+            for j in range(PACK):
+                nc.vector.tensor_tensor(g_raw[c, e, lo][:, j, :], planes[c, j][:].indirect(picks), gates[e][:, lo:hi], MULT)
+            g_bf[c, e, lo] = ring.tile([P, hi - lo, PACK], BF16, name="g_bf", bufs=4, align_bytes=64)
+            interleave(g_bf[c, e, lo], g_raw[c, e, lo])
+
+        def quantize_g(c, e, lo, hi):
+            if lo == 0:
+                g_mx[c, e] = mx_tiles(C, "g", 3)
+            quantize(g_mx[c, e][0][:, lo:hi], g_mx[c, e][1][:, lo:hi], g_bf[c, e, lo], E5M2)
+
+        def multiply(bank, weights, kt, moving, c):
+            cols = slice(kt * P, (kt + 1) * P)
+            nc.tensor.matmul_mx(
+                out=bank[:],
+                lhsT=weights[0][:, cols].bitcast(E4M3),
+                lhsT_scale=weights[1][:, cols],
+                rhs=moving[0][:].bitcast(E5M2),
+                rhs_scale=moving[1][:],
+                start=(c == 0),
+                stop=(c == PASSES - 1),
+            )
+
+        def multiply_routed(c, e):
+            for kt in range(K_TILES):
+                if c == 0:
+                    banks[e, kt] = psum.tile([P, C], F32, name="bank%d" % (e * K_TILES + kt))
+                multiply(banks[e, kt], w_mx[c, e], kt, g_mx[c, e], c)
+                if c == PASSES - 1:
+                    nc.scalar.copy(dx[kt][:, e * C : (e + 1) * C], banks[e, kt][:])
+
+        def multiply_shared(c, h):
+            for kt in range(K_TILES):
+                if c == 0:
+                    ds_banks[h, kt] = psum.tile([P, HALF], F32, name="bank%d" % (h * K_TILES + kt))
+                multiply(ds_banks[h, kt], w_mx[c, E], kt, s_mx[c, h], c)
+
+        nc.sync.dma_start(offs_t[:], offs)
+        load_plane(0, 0)
+        load_gate(0)
+        for j in range(1, PACK):
+            load_plane(0, j)
+        load_w(0, 0)
+        for e in range(1, E):
+            load_gate(e)
+            load_w(0, e)
+
+        units = [(c, e) for c in range(PASSES) for e in range(E)]
+        halves = [(c, h) for c in range(PASSES) for h in range(T // HALF)]
+        round_at = {1: 0, 2: 1, 4: 2, 5: 3, 7: 4}
+        load_at = {0: 0, 1: 1, 3: 2, 4: 3, 6: 4, 8: 5}
+        quantize_at = {3: 0, 4: 1}
+        last = len(units) - 1
+        round_w(0, 0)
+        for u, (c, e) in enumerate(units):
+            if u in load_at:
+                load_shared(*halves[load_at[u]])
+            if c + 1 < PASSES:
+                load_plane(c + 1, e)
+                load_w(c + 1, e)
+            if e == 2:
+                load_w(c, E)
+            if u == 2:
+                nc.sync.dma_start(pos1_t[:], pos1)
+                nc.sync.dma_start(pos2_t[:], pos2)
+            if u < last:
+                gather_g(c, e, 0, C)
+                round_w(*units[u + 1])
+            else:
+                gather_g(c, e, 0, C // 2)
+            if u in round_at:
+                round_shared(*halves[round_at[u]])
+            if e == 3:
+                round_w(c, E)
+            quantize_w(c, e)
+            if u >= 2:
+                quantize_g(*units[u - 2], 0, C)
+                multiply_routed(*units[u - 2])
+            if u in quantize_at:
+                quantize_shared(*halves[quantize_at[u]])
+
+        c, e = units[last]
+        gather_g(c, e, C // 2, C)
+        quantize_g(*units[last - 1], 0, C)
+        multiply_routed(*units[last - 1])
+        quantize_shared(*halves[2])
+        quantize_g(c, e, 0, C // 2)
+        quantize_shared(*halves[3])
+        quantize_g(c, e, C // 2, C)
+        multiply_routed(c, e)
+        round_shared(*halves[5])
+        for cs in range(PASSES):
+            quantize_w(cs, E)
+        quantize_shared(*halves[4])
+        for cs, h in halves[:5]:
+            multiply_shared(cs, h)
+
+        first = [keep.tile([P, T], F32, name="first%d" % kt) for kt in range(K_TILES)]
+        second = [keep.tile([P, T], F32, name="second%d" % kt) for kt in range(K_TILES)]
+
+        def cols(h):
+            return slice(h * HALF, (h + 1) * HALF)
+
+        def add_shared(kt, h):
+            nc.vector.tensor_tensor(first[kt][:, cols(h)], ds_banks[h, kt][:], first[kt][:, cols(h)], ADD)
+
+        def add_second(kt, h):
+            nc.vector.tensor_tensor(second[kt][:, cols(h)], first[kt][:, cols(h)], second[kt][:, cols(h)], ADD)
+            nc.sync.dma_start(out[kt * P : (kt + 1) * P, cols(h)], second[kt][:, cols(h)])
+
+        nc.vector.tensor_copy(first[0][:], dx[0][:].indirect(pos1_t[:]))
+        quantize_shared(*halves[5])
+        multiply_shared(*halves[5])
+        nc.vector.tensor_copy(second[0][:], dx[0][:].indirect(pos2_t[:]))
+        nc.vector.tensor_copy(first[1][:], dx[1][:].indirect(pos1_t[:]))
+        for h in range(2):
+            add_shared(0, h)
+        for h in range(2):
+            add_second(0, h)
+        for h in range(2):
+            add_shared(1, h)
+        for h in range(2):
+            picks = pos2_t[:, h * HALF // STRIPE : (h + 1) * HALF // STRIPE]
+            nc.vector.tensor_copy(second[1][:, cols(h)], dx[1][:].indirect(picks))
+        for h in range(2):
+            add_second(1, h)

@@ -4,6 +4,7 @@ import concourse.mybir as mybir
 
 K, T, E, C, N = 256, 1024, 4, 512, 1536
 SLOTS = E * C
+SHARED = E
 FLOPS = 2 * N * K * (SLOTS + T)
 BYTES = 4 * (N * T + (E + 1) * N * K + SLOTS + K * T) + 2 * 128 * (SLOTS + 2 * T) // 16
 
@@ -24,7 +25,29 @@ PASSES = N // PASS_ROWS
 K_TILES = K // P
 HALF = 512
 STRIPE = 16
-RUN = 4
+ALIGN = 64
+PAD = 32
+RUN = 2
+END = C // 2
+CUT = HALF // 2
+
+G_LAG = 2
+W_LEAD = 3
+EVERY = 3
+G_RAW_BUFS = 2
+G_BUFS = G_LAG + 1
+W_RAW_BUFS = 4
+W_BF_BUFS = 3
+W_MX_BUFS = W_LEAD + G_LAG + 1
+S_RAW_BUFS = 3
+
+PIECES = [(0, 0), (0, 1), (1, 0), (2, 0), (1, 1), (2, 1)]
+LATE = PIECES[3:]
+
+AFTER_LAST_BUT_ONE_G = "g_bf_mid"
+AFTER_LAST_G = "g_bf_end"
+AFTER_FIRST_PASS_OF_DS = "s_bf_wide"
+AFTER_ROUTED = ["g_end_codes", "w_end_codes", "g_end_scales"]
 
 
 def tile_moe_bds_lin_none_kernel(tc, dyT, w, gate, offs, pos1, pos2, out):
@@ -39,80 +62,104 @@ def tile_moe_bds_lin_none_kernel(tc, dyT, w, gate, offs, pos1, pos2, out):
         pos1_t = lists.tile([P, T // STRIPE], U16, name="pos1_t")
         pos2_t = lists.tile([P, T // STRIPE], U16, name="pos2_t")
         dx = [keep.tile([P, SLOTS], F32, name="dx%d" % kt) for kt in range(K_TILES)]
+        gate_t = keep.tile([P, SLOTS], F32, name="gate_t")
+        ws_bf = keep.tile([P, PASSES, K, PACK], BF16, name="ws_bf", align_bytes=ALIGN)
 
-        planes, gates, w_raw, w_bf, w_mx = {}, {}, {}, {}, {}
-        g_raw, g_bf, g_mx, banks = {}, {}, {}, {}
+        planes, w_raw, w_bf, w_mx = {}, {}, {}, {}
+        g_raw, g_bf, g_mx, dx_banks = {}, {}, {}, {}
         s_raw, s_bf, s_mx, ds_banks = {}, {}, {}, {}
 
         def pass_rows(mat, c):
-            return mat[c * PASS_ROWS : (c + 1) * PASS_ROWS, :].rearrange("(p j) x -> p j x", j=PACK)
+            return mat[c * PASS_ROWS : (c + 1) * PASS_ROWS, :]
 
         def load_plane(c, j):
-            planes[c, j] = ring.tile([P, T], F32, name="plane", bufs=8)
-            nc.sync.dma_start(planes[c, j][:], pass_rows(dyT, c)[:, j, :])
+            planes[c, j] = ring.tile([P, T + PAD], F32, name="plane%d_%d" % (c % 2, j))
+            rows = pass_rows(dyT, c).rearrange("(p j) x -> p (j x)", j=PACK)
+            if j + 1 < PACK:
+                nc.sync.dma_start(planes[c, j][:], rows[:, j * T : (j + 1) * T + PAD])
+            else:
+                nc.sync.dma_start(planes[c, j][:, T : T + PAD], rows[:, 0:PAD])
+                nc.sync.dma_start(planes[c, j][:, 0:T], rows[:, j * T : (j + 1) * T])
 
         def load_gate(e):
-            gates[e] = keep.tile([P, C], F32, name="gate%d" % e)
-            nc.sync.dma_start(gates[e][:], gate[0:P, e * C : (e + 1) * C])
+            nc.sync.dma_start(gate_t[:, e * C : (e + 1) * C], gate[0:P, e * C : (e + 1) * C])
 
         def load_w(c, e):
-            w_raw[c, e] = ring.tile([P, PACK, K], F32, name="w_raw", bufs=5)
-            nc.sync.dma_start(w_raw[c, e][:], pass_rows(w[e], c))
+            w_raw[c, e] = ring.tile([P, PACK, K], F32, name="w_raw", bufs=W_RAW_BUFS)
+            nc.sync.dma_start(w_raw[c, e][:], pass_rows(w[e], c).rearrange("(p j) x -> p j x", j=PACK))
 
         def load_shared(c, h):
-            s_raw[c, h] = ring.tile([P, PACK, HALF], F32, name="s_raw", bufs=2)
-            nc.sync.dma_start(s_raw[c, h][:], pass_rows(dyT, c)[:, :, h * HALF : (h + 1) * HALF])
+            s_raw[c, h] = ring.tile([P, PACK, HALF], F32, name="s_raw", bufs=S_RAW_BUFS)
+            rows = pass_rows(dyT, c).rearrange("(p j) x -> p j x", j=PACK)
+            nc.sync.dma_start(s_raw[c, h][:], rows[:, :, h * HALF : (h + 1) * HALF])
 
-        def interleave(dst, src):
+        def round_planes(dst, src):
             nc.scalar.copy(
-                dst[:].rearrange("p (c i) j -> p c j i", i=RUN),
-                src[:].rearrange("p j (c i) -> p c j i", i=RUN),
+                dst.rearrange("p (y i) j -> p y j i", i=RUN),
+                src.rearrange("p j (y i) -> p y j i", i=RUN),
             )
 
-        def quantize(codes, scales, src, fmt):
-            nc.vector.quantize_mx(out=codes.bitcast(fmt), scales=scales, in_=src[:].rearrange("p x j -> p (x j)"))
-
-        def mx_tiles(width, name, bufs):
-            codes = ring.tile([P, width], U32, name=name + "_codes", bufs=bufs, align_bytes=64)
-            scales = ring.tile([P, width], U8, name=name + "_scales", bufs=bufs, align_bytes=64)
+        def mx_tiles(width, codes_tag, scales_tag, codes_bufs=1, scales_bufs=1):
+            codes = ring.tile([P, width], U32, name=codes_tag, bufs=codes_bufs, align_bytes=ALIGN)
+            scales = ring.tile([P, width], U8, name=scales_tag, bufs=scales_bufs, align_bytes=ALIGN)
             return codes, scales
 
-        def round_w(c, e):
-            tag, bufs = ("ws_bf", PASSES) if e == E else ("w_bf", 3)
-            w_bf[c, e] = ring.tile([P, K, PACK], BF16, name=tag, bufs=bufs, align_bytes=64)
-            interleave(w_bf[c, e], w_raw[c, e])
+        def quantize(mx, lo, hi, flat_bf, fmt):
+            nc.vector.quantize_mx(out=mx[0][:, lo:hi].bitcast(fmt), scales=mx[1][:, lo:hi], in_=flat_bf)
 
-        def quantize_w(c, e):
-            w_mx[c, e] = mx_tiles(K, "ws", PASSES) if e == E else mx_tiles(K, "w", 3)
-            quantize(w_mx[c, e][0][:], w_mx[c, e][1][:], w_bf[c, e], E4M3)
+        def columns(mx, lo, hi):
+            return mx[0][:, lo:hi], mx[1][:, lo:hi]
 
-        def round_shared(c, h):
-            s_bf[c, h] = ring.tile([P, HALF, PACK], BF16, name="s_bf", bufs=4, align_bytes=64)
-            interleave(s_bf[c, h], s_raw[c, h])
+        def prepare_w(c, e):
+            w_bf[c, e] = ring.tile([P, K, PACK], BF16, name="w_bf", bufs=W_BF_BUFS, align_bytes=ALIGN)
+            round_planes(w_bf[c, e][:], w_raw[c, e][:])
+            if (c, e) == steps[last]:
+                w_mx[c, e] = mx_tiles(K, AFTER_ROUTED[1], "w_end_scales")
+            else:
+                w_mx[c, e] = mx_tiles(K, "w_codes", "w_scales", W_MX_BUFS, W_MX_BUFS)
+            quantize(w_mx[c, e], 0, K, w_bf[c, e][:].rearrange("p x j -> p (x j)"), E4M3)
 
-        def quantize_shared(c, h):
-            s_mx[c, h] = mx_tiles(HALF, "s", 2 * PASSES)
-            quantize(s_mx[c, h][0][:], s_mx[c, h][1][:], s_bf[c, h], E5M2)
+        def quantize_shared_w(codes_tag):
+            mx = mx_tiles(PASSES * K, codes_tag, "ws_scales")
+            flat = ws_bf[:].rearrange("p c x j -> p (c x j)")
+            for lo, hi in ((0, 2 * K), (2 * K, PASSES * K)):
+                quantize(mx, lo, hi, flat[:, lo * PACK : hi * PACK], E4M3)
+            for c in range(PASSES):
+                w_mx[c, SHARED] = columns(mx, c * K, (c + 1) * K)
 
-        def gather_g(c, e, lo, hi):
-            g_raw[c, e, lo] = ring.tile([P, PACK, hi - lo], F32, name="g_raw", bufs=3)
-            picks = offs_t[:, (e * C + lo) // STRIPE : (e * C + hi) // STRIPE]
-            for j in range(PACK):
-                nc.vector.tensor_tensor(g_raw[c, e, lo][:, j, :], planes[c, j][:].indirect(picks), gates[e][:, lo:hi], MULT)
-            g_bf[c, e, lo] = ring.tile([P, hi - lo, PACK], BF16, name="g_bf", bufs=4, align_bytes=64)
-            interleave(g_bf[c, e, lo], g_raw[c, e, lo])
+        def round_piece(c, h, tag):
+            s_bf[c, h] = ring.tile([P, HALF, PACK], BF16, name=tag, align_bytes=ALIGN)
+            round_planes(s_bf[c, h][:], s_raw[c, h][:])
+
+        def quantize_piece(c, h, codes_tag):
+            s_mx[c, h] = mx_tiles(HALF, codes_tag, "s_scales%d_%d" % (c, h))
+            quantize(s_mx[c, h], 0, HALF, s_bf[c, h][:].rearrange("p x j -> p (x j)"), E5M2)
+
+        def gather_g(c, lo, hi, j, cuts=1):
+            if j == 0:
+                tile = ring.tile([P, PACK, hi - lo], F32, name="g_raw", bufs=G_RAW_BUFS)
+                for first in range(lo, hi, END):
+                    g_raw[c, first] = tile, lo
+            tile = g_raw[c, lo][0]
+            width = (hi - lo) // cuts
+            for a in range(lo, hi, width):
+                window = planes[c, j][:].indirect(offs_t[:, a // STRIPE : (a + width) // STRIPE])
+                nc.vector.tensor_tensor(tile[:, j, a - lo : a - lo + width], window, gate_t[:, a : a + width], MULT)
+
+        def round_g(c, e, lo, hi, tag="g_bf", bufs=G_BUFS):
+            g_bf[c, e, lo] = ring.tile([P, hi - lo, PACK], BF16, name=tag, bufs=bufs, align_bytes=ALIGN)
+            tile, base = g_raw[c, e * C + lo]
+            round_planes(g_bf[c, e, lo][:], tile[:, :, e * C + lo - base : e * C + hi - base])
 
         def quantize_g(c, e, lo, hi):
-            if lo == 0:
-                g_mx[c, e] = mx_tiles(C, "g", 3)
-            quantize(g_mx[c, e][0][:, lo:hi], g_mx[c, e][1][:, lo:hi], g_bf[c, e, lo], E5M2)
+            quantize(g_mx[c, e], lo, hi, g_bf[c, e, lo][:].rearrange("p x j -> p (x j)"), E5M2)
 
         def multiply(bank, weights, kt, moving, c):
-            cols = slice(kt * P, (kt + 1) * P)
+            w_codes, w_scales = columns(weights, kt * P, (kt + 1) * P)
             nc.tensor.matmul_mx(
                 out=bank[:],
-                lhsT=weights[0][:, cols].bitcast(E4M3),
-                lhsT_scale=weights[1][:, cols],
+                lhsT=w_codes.bitcast(E4M3),
+                lhsT_scale=w_scales,
                 rhs=moving[0][:].bitcast(E5M2),
                 rhs_scale=moving[1][:],
                 start=(c == 0),
@@ -122,103 +169,146 @@ def tile_moe_bds_lin_none_kernel(tc, dyT, w, gate, offs, pos1, pos2, out):
         def multiply_routed(c, e):
             for kt in range(K_TILES):
                 if c == 0:
-                    banks[e, kt] = psum.tile([P, C], F32, name="bank%d" % (e * K_TILES + kt))
-                multiply(banks[e, kt], w_mx[c, e], kt, g_mx[c, e], c)
-                if c == PASSES - 1:
-                    nc.scalar.copy(dx[kt][:, e * C : (e + 1) * C], banks[e, kt][:])
+                    dx_banks[e, kt] = psum.tile([P, C], F32, name="bank%d" % (e * K_TILES + kt))
+                multiply(dx_banks[e, kt], w_mx[c, e], kt, g_mx[c, e], c)
 
-        def multiply_shared(c, h):
-            for kt in range(K_TILES):
-                if c == 0:
-                    ds_banks[h, kt] = psum.tile([P, HALF], F32, name="bank%d" % (h * K_TILES + kt))
-                multiply(ds_banks[h, kt], w_mx[c, E], kt, s_mx[c, h], c)
+        def finish_step(c, e):
+            g_mx[c, e] = mx_tiles(C, "g_codes", "g_scales", G_BUFS, G_BUFS)
+            quantize_g(c, e, 0, C)
+            multiply_routed(c, e)
 
-        nc.sync.dma_start(offs_t[:], offs)
+        def multiply_shared(c, h, kt):
+            if c == 0:
+                ds_banks[h, kt] = psum.tile([P, HALF], F32, name="bank%d" % ((E - 2 + h) * K_TILES + kt))
+            multiply(ds_banks[h, kt], w_mx[c, SHARED], kt, s_mx[c, h], c)
+
+        steps = [(c, e) for c in range(PASSES) for e in range(E)]
+        last = len(steps) - 1
+
         load_plane(0, 0)
+        nc.sync.dma_start(offs_t[:], offs)
         load_gate(0)
-        for j in range(1, PACK):
-            load_plane(0, j)
+        load_gate(1)
+        load_plane(0, 1)
         load_w(0, 0)
-        for e in range(1, E):
-            load_gate(e)
-            load_w(0, e)
+        load_plane(0, 2)
+        load_w(0, 1)
+        load_w(0, 2)
+        load_plane(0, 3)
+        load_w(0, 3)
+        load_gate(2)
+        load_gate(3)
+        for u in range(W_LEAD):
+            prepare_w(*steps[u])
+        for j in range(PACK):
+            gather_g(0, 0, 2 * C, j, cuts=2 if j == 0 else 1)
 
-        units = [(c, e) for c in range(PASSES) for e in range(E)]
-        halves = [(c, h) for c in range(PASSES) for h in range(T // HALF)]
-        round_at = {1: 0, 2: 1, 4: 2, 5: 3, 7: 4}
-        load_at = {0: 0, 1: 1, 3: 2, 4: 3, 6: 4, 8: 5}
-        quantize_at = {3: 0, 4: 1}
-        last = len(units) - 1
-        round_w(0, 0)
-        for u, (c, e) in enumerate(units):
-            if u in load_at:
-                load_shared(*halves[load_at[u]])
+        early = [piece for piece in PIECES if piece not in LATE]
+        piece_rounded_in = {EVERY * i: piece for i, piece in enumerate(early)}
+        load_steps = [max(0, u - 1) for u in piece_rounded_in] + list(range(len(steps) - len(LATE), len(steps)))
+        piece_loaded_in = dict(zip(load_steps, PIECES))
+        s_wide = ring.tile([P, T, PACK], BF16, name=AFTER_FIRST_PASS_OF_DS, align_bytes=ALIGN)
+
+        for u, (c, e) in enumerate(steps):
+            if c + 1 < PASSES and e < 2:
+                load_plane(c + 1, 2 * e)
+                load_plane(c + 1, 2 * e + 1)
+            if u in piece_loaded_in:
+                load_shared(*piece_loaded_in[u])
             if c + 1 < PASSES:
-                load_plane(c + 1, e)
                 load_w(c + 1, e)
-            if e == 2:
-                load_w(c, E)
-            if u == 2:
+            if u % EVERY == 0 and u // EVERY < PASSES:
+                load_w(u // EVERY, SHARED)
+            if (c, e) == (1, 1):
                 nc.sync.dma_start(pos1_t[:], pos1)
                 nc.sync.dma_start(pos2_t[:], pos2)
+
+            if u > 0 and e % 2 == 0:
+                hi = SLOTS - END if u == last - 1 else (e + 2) * C
+                for j in range(PACK):
+                    gather_g(c, e * C, hi, j)
             if u < last:
-                gather_g(c, e, 0, C)
-                round_w(*units[u + 1])
+                round_g(c, e, 0, C)
             else:
-                gather_g(c, e, 0, C // 2)
-            if u in round_at:
-                round_shared(*halves[round_at[u]])
-            if e == 3:
-                round_w(c, E)
-            quantize_w(c, e)
-            if u >= 2:
-                quantize_g(*units[u - 2], 0, C)
-                multiply_routed(*units[u - 2])
-            if u in quantize_at:
-                quantize_shared(*halves[quantize_at[u]])
+                round_g(c, e, 0, C - END, AFTER_LAST_BUT_ONE_G, 1)
+            if u >= G_LAG:
+                finish_step(*steps[u - G_LAG])
+            if u + W_LEAD <= last:
+                prepare_w(*steps[u + W_LEAD])
 
-        c, e = units[last]
-        gather_g(c, e, C // 2, C)
-        quantize_g(*units[last - 1], 0, C)
-        multiply_routed(*units[last - 1])
-        quantize_shared(*halves[2])
-        quantize_g(c, e, 0, C // 2)
-        quantize_shared(*halves[3])
-        quantize_g(c, e, C // 2, C)
+            if u in piece_rounded_in:
+                cs, h = piece_rounded_in[u]
+                if cs == 0:
+                    round_planes(s_wide[:, h * HALF : (h + 1) * HALF, :], s_raw[cs, h][:])
+                else:
+                    round_piece(cs, h, "s_bf")
+            if u % EVERY == 1 and u // EVERY < PASSES:
+                round_planes(ws_bf[:, u // EVERY, :, :], w_raw[u // EVERY, SHARED][:])
+
+        c, e = steps[last]
+        for j in range(PACK):
+            gather_g(c, SLOTS - END, SLOTS, j)
+        round_g(c, e, C - END, C, AFTER_LAST_G, 1)
+        finish_step(*steps[last - 1])
+        g_mx[c, e] = mx_tiles(C, AFTER_ROUTED[0], AFTER_ROUTED[2])
+        quantize_g(c, e, 0, C - END)
+        quantize_g(c, e, C - END, C)
         multiply_routed(c, e)
-        round_shared(*halves[5])
-        for cs in range(PASSES):
-            quantize_w(cs, E)
-        quantize_shared(*halves[4])
-        for cs, h in halves[:5]:
-            multiply_shared(cs, h)
+        for kt, experts in ((0, (0, 1, 2, 3)), (1, (2, 3, 0, 1))):
+            for done in experts:
+                nc.scalar.copy(dx[kt][:, done * C : (done + 1) * C], dx_banks[done, kt][:])
 
-        first = [keep.tile([P, T], F32, name="first%d" % kt) for kt in range(K_TILES)]
-        second = [keep.tile([P, T], F32, name="second%d" % kt) for kt in range(K_TILES)]
+        quantize_piece(1, 0, AFTER_LAST_BUT_ONE_G)
+        wide_mx = mx_tiles(T, AFTER_LAST_G, "s_wide_scales")
+        quantize(wide_mx, 0, T, s_wide[:].rearrange("p x j -> p (x j)"), E5M2)
+        for h in range(T // HALF):
+            s_mx[0, h] = columns(wide_mx, h * HALF, (h + 1) * HALF)
+        quantize_shared_w(AFTER_FIRST_PASS_OF_DS)
 
-        def cols(h):
-            return slice(h * HALF, (h + 1) * HALF)
+        for cs, h in early:
+            for kt in range(K_TILES):
+                multiply_shared(cs, h, kt)
+        for piece, tag in zip(LATE, AFTER_ROUTED):
+            round_piece(*piece, tag)
 
-        def add_shared(kt, h):
-            nc.vector.tensor_tensor(first[kt][:, cols(h)], ds_banks[h, kt][:], first[kt][:, cols(h)], ADD)
+        def fetch(kt, pos_t, lo, hi, tag):
+            part = ring.tile([P, hi - lo], F32, name=tag, align_bytes=ALIGN)
+            nc.vector.tensor_copy(part[:], dx[kt][:].indirect(pos_t[:, lo // STRIPE : hi // STRIPE]))
+            return part
 
-        def add_second(kt, h):
-            nc.vector.tensor_tensor(second[kt][:, cols(h)], first[kt][:, cols(h)], second[kt][:, cols(h)], ADD)
-            nc.sync.dma_start(out[kt * P : (kt + 1) * P, cols(h)], second[kt][:, cols(h)])
+        def finish_piece(c, h):
+            quantize_piece(c, h, "s_codes%d_%d" % (c, h))
+            for kt in reversed(range(K_TILES)):
+                multiply_shared(c, h, kt)
 
-        nc.vector.tensor_copy(first[0][:], dx[0][:].indirect(pos1_t[:]))
-        quantize_shared(*halves[5])
-        multiply_shared(*halves[5])
-        nc.vector.tensor_copy(second[0][:], dx[0][:].indirect(pos2_t[:]))
-        nc.vector.tensor_copy(first[1][:], dx[1][:].indirect(pos1_t[:]))
-        for h in range(2):
-            add_shared(0, h)
-        for h in range(2):
-            add_second(0, h)
-        for h in range(2):
-            add_shared(1, h)
-        for h in range(2):
-            picks = pos2_t[:, h * HALF // STRIPE : (h + 1) * HALF // STRIPE]
-            nc.vector.tensor_copy(second[1][:, cols(h)], dx[1][:].indirect(picks))
-        for h in range(2):
-            add_second(1, h)
+        def add_ds(kt, h, fetched):
+            summed = ring.tile([P, HALF], F32, name="summed%d_%d" % (kt, h))
+            nc.vector.tensor_tensor(summed[:], ds_banks[h, kt][:], fetched[:, h * HALF : (h + 1) * HALF], ADD)
+            return summed
+
+        def store(kt, lo, hi, part):
+            nc.sync.dma_start(out[kt * P : (kt + 1) * P, lo:hi], part)
+
+        first0 = fetch(0, pos1_t, 0, T, "first0")
+        both0 = fetch(0, pos2_t, 0, T, "both0")
+        finish_piece(*LATE[0])
+        for lo in range(0, T, HALF):
+            nc.gpsimd.tensor_tensor(both0[:, lo : lo + HALF], first0[:, lo : lo + HALF], both0[:, lo : lo + HALF], ADD)
+        first1 = fetch(1, pos1_t, 0, T, AFTER_ROUTED[0])
+
+        finish_piece(*LATE[1])
+        store(0, 0, HALF, add_ds(0, 0, both0)[:])
+        partial_low = add_ds(1, 0, first1)
+        second1_low = fetch(1, pos2_t, 0, HALF, AFTER_ROUTED[1])
+
+        finish_piece(*LATE[2])
+        nc.gpsimd.tensor_tensor(second1_low[:], partial_low[:], second1_low[:], ADD)
+        store(1, 0, HALF, second1_low[:])
+        second1_high = fetch(1, pos2_t, HALF, T, AFTER_ROUTED[2])
+
+        partial_high = add_ds(1, 1, first1)
+        store(0, HALF, T, add_ds(0, 1, both0)[:])
+        for lo in range(0, HALF, CUT):
+            part = second1_high[:, lo : lo + CUT]
+            nc.vector.tensor_tensor(part, partial_high[:, lo : lo + CUT], part, ADD)
+            store(1, HALF + lo, HALF + lo + CUT, part)

from contextlib import ExitStack

import concourse.mybir as mybir

K, T, E, C, N = 256, 1024, 4, 512, 1536
SLOTS = E * C
SHARED = E
FLOPS = 2 * N * K * (SLOTS + T)
BYTES = 4 * (N * T + (E + 1) * N * K + SLOTS + K * T) + 2 * 128 * (SLOTS + 2 * T) // 16

F32 = mybir.dt.float32
BF16 = mybir.dt.bfloat16
U32 = mybir.dt.uint32
U16 = mybir.dt.uint16
U8 = mybir.dt.uint8
E4M3 = mybir.dt.float8_e4m3fn_x4
E5M2 = mybir.dt.float8_e5m2_x4
MULT = mybir.AluOpType.mult
ADD = mybir.AluOpType.add

P = 128
PACK = 4
PASS_ROWS = P * PACK
PASSES = N // PASS_ROWS
K_TILES = K // P
HALF = 512
STRIPE = 16
ALIGN = 64
PAD = 32
RUN = 2
END = C // 2
CUT = HALF // 2

G_LAG = 2
W_LEAD = 3
EVERY = 3
G_RAW_BUFS = 2
G_BUFS = G_LAG + 1
W_RAW_BUFS = 4
W_BF_BUFS = 3
W_MX_BUFS = W_LEAD + G_LAG + 1
S_RAW_BUFS = 3

PIECES = [(0, 0), (0, 1), (1, 0), (2, 0), (1, 1), (2, 1)]
LATE = PIECES[3:]

AFTER_LAST_BUT_ONE_G = "g_bf_mid"
AFTER_LAST_G = "g_bf_end"
AFTER_FIRST_PASS_OF_DS = "s_bf_wide"
AFTER_ROUTED = ["g_end_codes", "w_end_codes", "g_end_scales"]


def tile_moe_bds_lin_none_kernel(tc, dyT, w, gate, offs, pos1, pos2, out):
    nc = tc.nc
    with ExitStack() as ctx:
        lists = ctx.enter_context(tc.tile_pool(name="lists", bufs=1))
        keep = ctx.enter_context(tc.tile_pool(name="keep", bufs=1))
        ring = ctx.enter_context(tc.tile_pool(name="ring", bufs=1))
        psum = ctx.enter_context(tc.psum_pool(name="psum", bufs=1))

        offs_t = lists.tile([P, SLOTS // STRIPE], U16, name="offs_t")
        pos1_t = lists.tile([P, T // STRIPE], U16, name="pos1_t")
        pos2_t = lists.tile([P, T // STRIPE], U16, name="pos2_t")
        dx = [keep.tile([P, SLOTS], F32, name="dx%d" % kt) for kt in range(K_TILES)]
        gate_t = keep.tile([P, SLOTS], F32, name="gate_t")
        ws_bf = keep.tile([P, PASSES, K, PACK], BF16, name="ws_bf", align_bytes=ALIGN)

        planes, w_raw, w_bf, w_mx = {}, {}, {}, {}
        g_raw, g_bf, g_mx, dx_banks = {}, {}, {}, {}
        s_raw, s_bf, s_mx, ds_banks = {}, {}, {}, {}

        def pass_rows(mat, c):
            return mat[c * PASS_ROWS : (c + 1) * PASS_ROWS, :]

        def load_plane(c, j):
            planes[c, j] = ring.tile([P, T + PAD], F32, name="plane%d_%d" % (c % 2, j))
            rows = pass_rows(dyT, c).rearrange("(p j) x -> p (j x)", j=PACK)
            if j + 1 < PACK:
                nc.sync.dma_start(planes[c, j][:], rows[:, j * T : (j + 1) * T + PAD])
            else:
                nc.sync.dma_start(planes[c, j][:, T : T + PAD], rows[:, 0:PAD])
                nc.sync.dma_start(planes[c, j][:, 0:T], rows[:, j * T : (j + 1) * T])

        def load_gate(e):
            nc.sync.dma_start(gate_t[:, e * C : (e + 1) * C], gate[0:P, e * C : (e + 1) * C])

        def load_w(c, e):
            w_raw[c, e] = ring.tile([P, PACK, K], F32, name="w_raw", bufs=W_RAW_BUFS)
            nc.sync.dma_start(w_raw[c, e][:], pass_rows(w[e], c).rearrange("(p j) x -> p j x", j=PACK))

        def load_shared(c, h):
            s_raw[c, h] = ring.tile([P, PACK, HALF], F32, name="s_raw", bufs=S_RAW_BUFS)
            rows = pass_rows(dyT, c).rearrange("(p j) x -> p j x", j=PACK)
            nc.sync.dma_start(s_raw[c, h][:], rows[:, :, h * HALF : (h + 1) * HALF])

        def round_planes(dst, src):
            nc.scalar.copy(
                dst.rearrange("p (y i) j -> p y j i", i=RUN),
                src.rearrange("p j (y i) -> p y j i", i=RUN),
            )

        def mx_tiles(width, codes_tag, scales_tag, codes_bufs=1, scales_bufs=1):
            codes = ring.tile([P, width], U32, name=codes_tag, bufs=codes_bufs, align_bytes=ALIGN)
            scales = ring.tile([P, width], U8, name=scales_tag, bufs=scales_bufs, align_bytes=ALIGN)
            return codes, scales

        def quantize(mx, lo, hi, flat_bf, fmt):
            nc.vector.quantize_mx(out=mx[0][:, lo:hi].bitcast(fmt), scales=mx[1][:, lo:hi], in_=flat_bf)

        def columns(mx, lo, hi):
            return mx[0][:, lo:hi], mx[1][:, lo:hi]

        def prepare_w(c, e):
            w_bf[c, e] = ring.tile([P, K, PACK], BF16, name="w_bf", bufs=W_BF_BUFS, align_bytes=ALIGN)
            round_planes(w_bf[c, e][:], w_raw[c, e][:])
            if (c, e) == steps[last]:
                w_mx[c, e] = mx_tiles(K, AFTER_ROUTED[1], "w_end_scales")
            else:
                w_mx[c, e] = mx_tiles(K, "w_codes", "w_scales", W_MX_BUFS, W_MX_BUFS)
            quantize(w_mx[c, e], 0, K, w_bf[c, e][:].rearrange("p x j -> p (x j)"), E4M3)

        def quantize_shared_w(codes_tag):
            mx = mx_tiles(PASSES * K, codes_tag, "ws_scales")
            flat = ws_bf[:].rearrange("p c x j -> p (c x j)")
            for lo, hi in ((0, 2 * K), (2 * K, PASSES * K)):
                quantize(mx, lo, hi, flat[:, lo * PACK : hi * PACK], E4M3)
            for c in range(PASSES):
                w_mx[c, SHARED] = columns(mx, c * K, (c + 1) * K)

        def round_piece(c, h, tag):
            s_bf[c, h] = ring.tile([P, HALF, PACK], BF16, name=tag, align_bytes=ALIGN)
            round_planes(s_bf[c, h][:], s_raw[c, h][:])

        def quantize_piece(c, h, codes_tag):
            s_mx[c, h] = mx_tiles(HALF, codes_tag, "s_scales%d_%d" % (c, h))
            quantize(s_mx[c, h], 0, HALF, s_bf[c, h][:].rearrange("p x j -> p (x j)"), E5M2)

        def gather_g(c, lo, hi, j, cuts=1):
            if j == 0:
                tile = ring.tile([P, PACK, hi - lo], F32, name="g_raw", bufs=G_RAW_BUFS)
                for first in range(lo, hi, END):
                    g_raw[c, first] = tile, lo
            tile = g_raw[c, lo][0]
            width = (hi - lo) // cuts
            for a in range(lo, hi, width):
                window = planes[c, j][:].indirect(offs_t[:, a // STRIPE : (a + width) // STRIPE])
                nc.vector.tensor_tensor(tile[:, j, a - lo : a - lo + width], window, gate_t[:, a : a + width], MULT)

        def round_g(c, e, lo, hi, tag="g_bf", bufs=G_BUFS):
            g_bf[c, e, lo] = ring.tile([P, hi - lo, PACK], BF16, name=tag, bufs=bufs, align_bytes=ALIGN)
            tile, base = g_raw[c, e * C + lo]
            round_planes(g_bf[c, e, lo][:], tile[:, :, e * C + lo - base : e * C + hi - base])

        def quantize_g(c, e, lo, hi):
            quantize(g_mx[c, e], lo, hi, g_bf[c, e, lo][:].rearrange("p x j -> p (x j)"), E5M2)

        def multiply(bank, weights, kt, moving, c):
            w_codes, w_scales = columns(weights, kt * P, (kt + 1) * P)
            nc.tensor.matmul_mx(
                out=bank[:],
                lhsT=w_codes.bitcast(E4M3),
                lhsT_scale=w_scales,
                rhs=moving[0][:].bitcast(E5M2),
                rhs_scale=moving[1][:],
                start=(c == 0),
                stop=(c == PASSES - 1),
            )

        def multiply_routed(c, e):
            for kt in range(K_TILES):
                if c == 0:
                    dx_banks[e, kt] = psum.tile([P, C], F32, name="bank%d" % (e * K_TILES + kt))
                multiply(dx_banks[e, kt], w_mx[c, e], kt, g_mx[c, e], c)

        def finish_step(c, e):
            g_mx[c, e] = mx_tiles(C, "g_codes", "g_scales", G_BUFS, G_BUFS)
            quantize_g(c, e, 0, C)
            multiply_routed(c, e)

        def multiply_shared(c, h, kt):
            if c == 0:
                ds_banks[h, kt] = psum.tile([P, HALF], F32, name="bank%d" % ((E - 2 + h) * K_TILES + kt))
            multiply(ds_banks[h, kt], w_mx[c, SHARED], kt, s_mx[c, h], c)

        steps = [(c, e) for c in range(PASSES) for e in range(E)]
        last = len(steps) - 1

        load_plane(0, 0)
        nc.sync.dma_start(offs_t[:], offs)
        load_gate(0)
        load_gate(1)
        load_plane(0, 1)
        load_w(0, 0)
        load_plane(0, 2)
        load_w(0, 1)
        load_w(0, 2)
        load_plane(0, 3)
        load_w(0, 3)
        load_gate(2)
        load_gate(3)
        for u in range(W_LEAD):
            prepare_w(*steps[u])
        for j in range(PACK):
            gather_g(0, 0, 2 * C, j, cuts=2 if j == 0 else 1)

        early = [piece for piece in PIECES if piece not in LATE]
        piece_rounded_in = {EVERY * i: piece for i, piece in enumerate(early)}
        load_steps = [max(0, u - 1) for u in piece_rounded_in] + list(range(len(steps) - len(LATE), len(steps)))
        piece_loaded_in = dict(zip(load_steps, PIECES))
        s_wide = ring.tile([P, T, PACK], BF16, name=AFTER_FIRST_PASS_OF_DS, align_bytes=ALIGN)

        for u, (c, e) in enumerate(steps):
            if c + 1 < PASSES and e < 2:
                load_plane(c + 1, 2 * e)
                load_plane(c + 1, 2 * e + 1)
            if u in piece_loaded_in:
                load_shared(*piece_loaded_in[u])
            if c + 1 < PASSES:
                load_w(c + 1, e)
            if u % EVERY == 0 and u // EVERY < PASSES:
                load_w(u // EVERY, SHARED)
            if (c, e) == (1, 1):
                nc.sync.dma_start(pos1_t[:], pos1)
                nc.sync.dma_start(pos2_t[:], pos2)

            if u > 0 and e % 2 == 0:
                hi = SLOTS - END if u == last - 1 else (e + 2) * C
                for j in range(PACK):
                    gather_g(c, e * C, hi, j)
            if u < last:
                round_g(c, e, 0, C)
            else:
                round_g(c, e, 0, C - END, AFTER_LAST_BUT_ONE_G, 1)
            if u >= G_LAG:
                finish_step(*steps[u - G_LAG])
            if u + W_LEAD <= last:
                prepare_w(*steps[u + W_LEAD])

            if u in piece_rounded_in:
                cs, h = piece_rounded_in[u]
                if cs == 0:
                    round_planes(s_wide[:, h * HALF : (h + 1) * HALF, :], s_raw[cs, h][:])
                else:
                    round_piece(cs, h, "s_bf")
            if u % EVERY == 1 and u // EVERY < PASSES:
                round_planes(ws_bf[:, u // EVERY, :, :], w_raw[u // EVERY, SHARED][:])

        c, e = steps[last]
        for j in range(PACK):
            gather_g(c, SLOTS - END, SLOTS, j)
        round_g(c, e, C - END, C, AFTER_LAST_G, 1)
        finish_step(*steps[last - 1])
        g_mx[c, e] = mx_tiles(C, AFTER_ROUTED[0], AFTER_ROUTED[2])
        quantize_g(c, e, 0, C - END)
        quantize_g(c, e, C - END, C)
        multiply_routed(c, e)
        for kt, experts in ((0, (0, 1, 2, 3)), (1, (2, 3, 0, 1))):
            for done in experts:
                nc.scalar.copy(dx[kt][:, done * C : (done + 1) * C], dx_banks[done, kt][:])

        quantize_piece(1, 0, AFTER_LAST_BUT_ONE_G)
        wide_mx = mx_tiles(T, AFTER_LAST_G, "s_wide_scales")
        quantize(wide_mx, 0, T, s_wide[:].rearrange("p x j -> p (x j)"), E5M2)
        for h in range(T // HALF):
            s_mx[0, h] = columns(wide_mx, h * HALF, (h + 1) * HALF)
        quantize_shared_w(AFTER_FIRST_PASS_OF_DS)

        for cs, h in early:
            for kt in range(K_TILES):
                multiply_shared(cs, h, kt)
        for piece, tag in zip(LATE, AFTER_ROUTED):
            round_piece(*piece, tag)

        def fetch(kt, pos_t, lo, hi, tag):
            part = ring.tile([P, hi - lo], F32, name=tag, align_bytes=ALIGN)
            nc.vector.tensor_copy(part[:], dx[kt][:].indirect(pos_t[:, lo // STRIPE : hi // STRIPE]))
            return part

        def finish_piece(c, h):
            quantize_piece(c, h, "s_codes%d_%d" % (c, h))
            for kt in reversed(range(K_TILES)):
                multiply_shared(c, h, kt)

        def add_ds(kt, h, fetched):
            summed = ring.tile([P, HALF], F32, name="summed%d_%d" % (kt, h))
            nc.vector.tensor_tensor(summed[:], ds_banks[h, kt][:], fetched[:, h * HALF : (h + 1) * HALF], ADD)
            return summed

        def store(kt, lo, hi, part):
            nc.sync.dma_start(out[kt * P : (kt + 1) * P, lo:hi], part)

        first0 = fetch(0, pos1_t, 0, T, "first0")
        both0 = fetch(0, pos2_t, 0, T, "both0")
        finish_piece(*LATE[0])
        for lo in range(0, T, HALF):
            nc.gpsimd.tensor_tensor(both0[:, lo : lo + HALF], first0[:, lo : lo + HALF], both0[:, lo : lo + HALF], ADD)
        first1 = fetch(1, pos1_t, 0, T, AFTER_ROUTED[0])

        finish_piece(*LATE[1])
        store(0, 0, HALF, add_ds(0, 0, both0)[:])
        partial_low = add_ds(1, 0, first1)
        second1_low = fetch(1, pos2_t, 0, HALF, AFTER_ROUTED[1])

        finish_piece(*LATE[2])
        nc.gpsimd.tensor_tensor(second1_low[:], partial_low[:], second1_low[:], ADD)
        store(1, 0, HALF, second1_low[:])
        second1_high = fetch(1, pos2_t, HALF, T, AFTER_ROUTED[2])

        partial_high = add_ds(1, 1, first1)
        store(0, HALF, T, add_ds(0, 1, both0)[:])
        for lo in range(0, HALF, CUT):
            part = second1_high[:, lo : lo + CUT]
            nc.vector.tensor_tensor(part, partial_high[:, lo : lo + CUT], part, ADD)
            store(1, HALF + lo, HALF + lo + CUT, part)
